import numpy as np
import ml_dtypes


def mxq(x, axis, fmt="e4m3"):
    dtype, down = {"e4m3": (ml_dtypes.float8_e4m3fn, 7), "e5m2": (ml_dtypes.float8_e5m2, 14)}[fmt]
    v = np.moveaxis(np.asarray(x, np.float32).astype(ml_dtypes.bfloat16).astype(np.float64), axis, -1)
    blocks = v.reshape(v.shape[:-1] + (-1, 32))
    amax = np.abs(blocks).max(-1, keepdims=True)
    byte = np.maximum(np.where(amax > 0, np.frexp(amax)[1] - 1 + 127, 0) - down, 1)
    scale = np.exp2(byte - 127.0)
    codes = (blocks / scale).astype(np.float32).astype(dtype).astype(np.float64)
    return np.moveaxis((codes * scale).reshape(v.shape), -1, axis)


WIDE = False


def mx_kscale(k):
    if not WIDE:
        return np.ones(k)
    levels = np.array([10, -10, 5, -5, 0])
    if k % 512:
        return np.exp2(np.random.permutation(np.resize(levels, k // 32))).repeat(32)
    a = np.empty((k // 512, 16))
    for p in range(k // 512):
        a[p, :8] = np.random.permutation(np.resize(levels, 8))
        for g in range(8):
            far = levels[np.abs(levels - a[p, g]) >= 10]
            a[p, g + 8] = far[np.random.randint(len(far))]
    return np.exp2(a.ravel()).repeat(32)


def f64(x):
    return np.asarray(x).astype(np.float64)


def striped(idx):
    return np.tile(idx.reshape(-1, 16).T, (8, 1)).astype(np.uint16)


def unstriped(offs):
    return offs[:16].T.reshape(-1).astype(np.int64)


def striped8(idx):
    return np.concatenate([x.reshape(-1, 16).T for x in idx]).astype(np.uint16)


def runs(offs, k):
    lists = np.stack([offs[16 * r : 16 * r + 16].T.reshape(-1) for r in range(8)]).astype(np.int64)
    return lists[np.arange(k) % 512 // 64]


def pack_weight(w):
    k, n = w.shape
    w = f64(np.asarray(w, np.float32).astype(ml_dtypes.bfloat16)).reshape(k // 32, 32, n)
    amax = np.abs(w).max(1)
    byte = np.clip(np.where(amax > 0, np.frexp(amax)[1] - 1 + 127 - 7, 1), 1, 254)
    scaled = (w * np.exp2(127.0 - byte)[:, None, :]).reshape(k, n).astype(np.float32)
    words = np.ascontiguousarray(scaled.reshape(k // 512, 128, 4, n).transpose(0, 1, 3, 2)).astype(ml_dtypes.float8_e4m3fn).view(np.uint8)
    return words, np.ascontiguousarray(byte.astype(np.uint8).reshape(k // 512, 16, n))


def unpack_weight(words, scales):
    g, p, n, _ = words.shape
    vals = np.ascontiguousarray(words).view(ml_dtypes.float8_e4m3fn).astype(np.float64) * np.repeat(np.exp2(scales.astype(np.float64) - 127.0), 8, axis=1)[..., None]
    return vals.transpose(0, 1, 3, 2).reshape(g * 512, n)


K, T, S, H = 512, 2048, 512, 512


def setup_inputs():
    n = np.random.standard_normal
    s = mx_kscale(K)[:, None]
    u = mx_kscale(S)
    packed_xT = pack_weight(n((K, T)) * s)
    return {
        "x_words": packed_xT[0],
        "x_scales": packed_xT[1],
        "wa": (n((K, H)) / np.sqrt(K) / s).astype(np.float32),
        "wb": (n((K, H)) / np.sqrt(K) / s).astype(np.float32),
        "gt": (np.random.uniform(0.5, 1.5, (S, 1)) * u[:, None]).astype(np.float32),
        "gi": (np.random.uniform(0.5, 1.5, (S, 1)) / u[:, None]).astype(np.float32),
        "offs": striped(np.random.permutation(T)[:S]),
        "two": striped(np.random.permutation(T)[:S]),
        "n1": striped(np.random.permutation(H)),
        "n2": striped(np.random.permutation(H)),
        "n3": striped8(np.stack([np.random.permutation(H) for _ in range(8)])),
        "n4": striped8(np.stack([np.random.permutation(H) for _ in range(8)])),
    }


def reference(x_words, x_scales, wa, wb, gt, gi, offs, two, n1, n2, n3, n4):
    xq = unpack_weight(x_words, x_scales)[:, unstriped(offs)]
    a = xq.T @ mxq(f64(wa), 0, "e4m3")
    x_two = unpack_weight(x_words, x_scales)[:, unstriped(two)]
    b = x_two.T @ mxq(f64(wb), 0, "e4m3")
    z = f64(gt) * (np.maximum(a, b[:, unstriped(n2)]) - (np.minimum(a[:, unstriped(n1)], b)))
    z2 = f64(gi) * b
    cv = 0.0625 * ((mxq(z, 0, "e4m3").T @ mxq(z2, 0, "e4m3")))
    return np.maximum(cv[np.arange(H)[:, None], runs(n3, H)], cv[np.arange(H)[:, None], runs(n4, H)]) - (0.75 * cv)

@@ -1,0 +1,222 @@
+from contextlib import ExitStack
+
+import concourse.mybir as mybir
+
+K, T, S, H = 512, 2048, 512, 512
+FLOPS = 3 * 2 * 512 * 512 * 512
+
+F32 = mybir.dt.float32
+BF16 = mybir.dt.bfloat16
+I32 = mybir.dt.int32
+U32 = mybir.dt.uint32
+U16 = mybir.dt.uint16
+U8 = mybir.dt.uint8
+FP8X4 = mybir.dt.float8_e4m3fn_x4
+ALU = mybir.AluOpType
+COPY = mybir.ActivationFunctionType.Copy
+
+P = 128
+PACK = 4
+HALF = 256
+HALF_COLS = HALF // 16
+
+
+def tile_picked_momtmaxbover_none_p_kernel(tc, x_words, x_scales, wa, wb, gt, gi, offs, two, n1, n2, n3, n4, out):
+    nc = tc.nc
+    with ExitStack() as ctx:
+        keep = ctx.enter_context(tc.tile_pool(name="keep", bufs=1))
+        psum = ctx.enter_context(tc.psum_pool(name="psum", bufs=1))
+
+        def sb(name, shape, dtype):
+            return keep.tile(shape, dtype, name=name, align_bytes=64)
+
+        def load_list(name, src):
+            t = keep.tile([P, S // 16], U16, name=name)
+            nc.sync.dma_start(t[:], src)
+            return t
+
+        def gather(engine, dst, window, lst, half):
+            cols = slice(half * HALF, (half + 1) * HALF)
+            picked = window.indirect(lst[:, half * HALF_COLS : (half + 1) * HALF_COLS])
+            if engine is nc.scalar:
+                nc.scalar.activation(dst[:, cols], picked, COPY)
+            else:
+                nc.vector.tensor_copy(dst[:, cols], picked)
+
+        xs = sb("xs", [P, T], U8)
+        nc.vector.memset(xs[:].bitcast(I32), 0)
+        two_t = load_list("two_t", two)
+        offs_t = load_list("offs_t", offs)
+        for q in range(4):
+            nc.scalar.dma_start(xs[32 * q : 32 * q + 4, :].bitcast(I32), x_scales[0, 4 * q : 4 * q + 4, :].bitcast(I32))
+
+        def load_weight(name, w):
+            halves = []
+            for h in range(2):
+                raw = sb(name + "_raw%d" % h, [P, PACK, HALF], F32)
+                nc.sync.dma_start(raw[:], w.rearrange("(p j) n -> p j n", j=PACK)[:, :, h * HALF : (h + 1) * HALF])
+                halves.append(raw)
+            return halves
+
+        wb_raw = load_weight("wb", wb)
+        xw = sb("xw", [P, T], U32)
+        nc.sync.dma_start(xw[:].bitcast(I32), x_words[0].rearrange("p n t -> p (n t)").bitcast(I32))
+        n2_t = load_list("n2_t", n2)
+        n1_t = load_list("n1_t", n1)
+        wa_raw = load_weight("wa", wa)
+        gt_t = sb("gt_t", [P, PACK], F32)
+        gi_t = sb("gi_t", [P, PACK], F32)
+        nc.scalar.dma_start(gt_t[:], gt.rearrange("(p j) o -> p (j o)", j=PACK))
+        nc.scalar.dma_start(gi_t[:], gi.rearrange("(p j) o -> p (j o)", j=PACK))
+        n3_t = load_list("n3_t", n3)
+        n4_t = load_list("n4_t", n4)
+
+        twice = sb("twice", [P, PACK], F32)
+        sign = sb("sign", [P, PACK], F32)
+        gt_abs = sb("gt_abs", [P, PACK], F32)
+        gi_signed = sb("gi_signed", [P, PACK], F32)
+        nc.gpsimd.tensor_scalar(twice[:], gt_t[:], 0.0, 2.0, ALU.is_ge, ALU.mult)
+        nc.gpsimd.tensor_scalar(sign[:], twice[:], 1.0, -1.0, ALU.mult, ALU.add)
+        nc.gpsimd.tensor_tensor(gt_abs[:], gt_t[:], sign[:], ALU.mult)
+        nc.gpsimd.tensor_tensor(gi_signed[:], gi_t[:], sign[:], ALU.mult)
+
+        def pick_scales(name, lst):
+            listed = sb(name + "_listed", [P, S], U8)
+            nc.vector.tensor_copy(listed[:], xs[:].indirect(lst[:]))
+            return listed
+
+        def deal_scales(name, listed):
+            dealt = sb(name + "_dealt", [P, S], U8)
+            nc.vector.tensor_copy(
+                dealt[:].rearrange("p (j m) -> p j m", j=PACK),
+                listed[:].rearrange("p (m j) -> p j m", j=PACK),
+            )
+            return dealt
+
+        def pick_words(name, lst):
+            dealt = sb(name, [P, S], U32)
+            nc.vector.tensor_copy(dealt[:].rearrange("p (j m) -> p m j", j=PACK), xw[:].indirect(lst[:]))
+            return dealt
+
+        def weave_weight(engine, woven, raw, h):
+            dst = woven[:, h * HALF * PACK : (h + 1) * HALF * PACK].rearrange("p (c e j) -> p c j e", e=4, j=PACK)
+            src = raw[:].rearrange("p j (c e) -> p c j e", e=4)
+            if engine is nc.scalar:
+                nc.scalar.copy(dst, src)
+            else:
+                nc.vector.tensor_copy(dst, src)
+
+        def quantize(codes, scales, woven):
+            nc.vector.quantize_mx(out=codes.bitcast(FP8X4), scales=scales, in_=woven)
+
+        def product(acc, lhs_codes, lhs_scales, rhs_codes, rhs_scales):
+            nc.tensor.matmul_mx(
+                out=acc, lhsT=lhs_codes.bitcast(FP8X4), lhsT_scale=lhs_scales,
+                rhs=rhs_codes.bitcast(FP8X4), rhs_scale=rhs_scales, start=True, stop=True,
+            )
+
+        two_listed = pick_scales("two_sc", two_t)
+        offs_listed = pick_scales("offs_sc", offs_t)
+        two_sc = deal_scales("two_sc", two_listed)
+        offs_sc = deal_scales("offs_sc", offs_listed)
+        wb_woven = sb("wb_woven", [P, H * PACK], BF16)
+        for h in range(2):
+            weave_weight(nc.scalar, wb_woven, wb_raw[h], h)
+        wb_codes = sb("wb_codes", [P, H], U32)
+        wb_scales = sb("wb_scales", [P, H], U8)
+        quantize(wb_codes[:], wb_scales[:], wb_woven[:])
+        two_w = pick_words("two_w", two_t)
+        b_ps = []
+        for j in range(PACK):
+            acc = psum.tile([P, H], F32, name="b_ps%d" % j)
+            cols = slice(j * P, (j + 1) * P)
+            product(acc[:], two_w[:, cols], two_sc[:, cols], wb_codes[:], wb_scales[:])
+            b_ps.append(acc)
+        offs_w = pick_words("offs_w", offs_t)
+        b_sb = sb("b_sb", [P, PACK, H], F32)
+        for j in range(PACK):
+            nc.scalar.copy(b_sb[:, j, :], b_ps[j][:])
+
+        wa_woven = sb("wa_woven", [P, H * PACK], BF16)
+        for h in range(2):
+            weave_weight(nc.vector, wa_woven, wa_raw[h], h)
+        wa_codes = sb("wa_codes", [P, H], U32)
+        wa_scales = sb("wa_scales", [P, H], U8)
+        quantize(wa_codes[:], wa_scales[:], wa_woven[:])
+        a_ps = []
+        for j in range(PACK):
+            acc = psum.tile([P, H], F32, name="a_ps%d" % j, tag="bank%d" % j)
+            cols = slice(j * P, (j + 1) * P)
+            product(acc[:], offs_w[:, cols], offs_sc[:, cols], wa_codes[:], wa_scales[:])
+            a_ps.append(acc)
+
+        b_at = [sb("b_at%d" % j, [P, H], F32) for j in range(PACK)]
+        for j in range(PACK):
+            for h in range(2):
+                gather(nc.scalar, b_at[j], b_sb[:, j, :], n2_t, h)
+
+        z2_woven = sb("z2_woven", [P, H * PACK], BF16)
+        nc.vector.tensor_tensor(
+            z2_woven[:].rearrange("p (c e j) -> p c j e", e=4, j=PACK),
+            b_sb[:].rearrange("p j (c e) -> p c j e", e=4),
+            gi_signed[:].unsqueeze(1).unsqueeze(3).to_broadcast([P, H // 4, PACK, 4]),
+            ALU.mult,
+        )
+        a_sb = [sb("a_sb%d" % j, [P, H], F32) for j in range(PACK)]
+        for j in range(PACK):
+            nc.vector.tensor_scalar(a_sb[j][:], a_ps[j][:], gt_abs[:, j : j + 1], None, ALU.mult)
+        z2_codes = sb("z2_codes", [P, H], U32)
+        z2_scales = sb("z2_scales", [P, H], U8)
+        quantize(z2_codes[:], z2_scales[:], z2_woven[:])
+
+        a_at = [sb("a_at%d" % j, [P, H], F32) for j in range(PACK)]
+        upper = sb("upper", [P, PACK, H], F32)
+        lower = sb("lower", [P, PACK, H], F32)
+        for j in range(PACK):
+            nc.vector.scalar_tensor_tensor(upper[:, j, :], b_at[j][:], gt_abs[:, j : j + 1], a_sb[j][:], ALU.mult, ALU.max)
+        for j in range(PACK):
+            for h in range(2):
+                gather(nc.scalar, a_at[j], a_sb[j][:], n1_t, h)
+            nc.vector.scalar_tensor_tensor(lower[:, j, :], b_ps[j][:], gt_abs[:, j : j + 1], a_at[j][:], ALU.mult, ALU.min)
+
+        z_woven = [sb("z_woven%d" % t, [P, P * PACK], BF16) for t in range(4)]
+        z_codes = [sb("z_codes%d" % t, [P, P], U32) for t in range(4)]
+        z_scales = [sb("z_scales%d" % t, [P, P], U8) for t in range(4)]
+        cv_ps = []
+
+        def weave_z(t):
+            nc.vector.tensor_tensor(
+                z_woven[t][:].rearrange("p (c e j) -> p c j e", e=4, j=PACK),
+                upper[:].rearrange("p j (c t e) -> p t c j e", t=4, e=4)[:, t],
+                lower[:].rearrange("p j (c t e) -> p t c j e", t=4, e=4)[:, t],
+                ALU.subtract,
+            )
+
+        def moments(t):
+            quantize(z_codes[t][:], z_scales[t][:], z_woven[t][:])
+            acc = psum.tile([P, H], F32, name="cv_ps%d" % t, tag="bank%d" % t)
+            product(acc[:], z_codes[t][:], z_scales[t][:], z2_codes[:], z2_scales[:])
+            cv_ps.append(acc)
+
+        weave_z(0)
+        for t in range(1, 4):
+            weave_z(t)
+            moments(t - 1)
+        moments(3)
+
+        out_rows = out.rearrange("(c t e) n -> t c e n", t=4, e=4)
+        on_vector = [0, 1, 2, 2]
+        for t in range(4):
+            cv = sb("cv%d" % t, [P, H], F32)
+            nc.scalar.activation(cv[:], cv_ps[t][:], COPY, scale=0.0625)
+            at3 = sb("at3_%d" % t, [P, H], F32)
+            at4 = sb("at4_%d" % t, [P, H], F32)
+            for h in range(2):
+                gather(nc.scalar, at3, cv[:], n3_t, h)
+            for h in range(2):
+                gather(nc.vector if h < on_vector[t] else nc.scalar, at4, cv[:], n4_t, h)
+            top = sb("top%d" % t, [P, H], F32)
+            nc.vector.tensor_tensor(top[:], at3[:], at4[:], ALU.max)
+            res = sb("res%d" % t, [P, H], F32)
+            nc.vector.scalar_tensor_tensor(res[:], cv_ps[t][:], -0.75 * 0.0625, top[:], ALU.mult, ALU.add)
+            nc.sync.dma_start(out_rows[t], res[:])

@@ -18,7 +18,7 @@ COPY = mybir.ActivationFunctionType.Copy
 P = 128
 PACK = 4
 HALF = 256
-HALF_COLS = HALF // 16
+WHOLE, LEFT, RIGHT = slice(0, H), slice(0, HALF), slice(HALF, H)
 
 
 def tile_picked_momtmaxbover_none_p_kernel(tc, x_words, x_scales, wa, wb, gt, gi, offs, two, n1, n2, n3, n4, out):
@@ -35,20 +35,26 @@ def tile_picked_momtmaxbover_none_p_kernel(tc, x_words, x_scales, wa, wb, gt, gi
             nc.sync.dma_start(t[:], src)
             return t
 
-        def gather(engine, dst, window, lst, half):
-            cols = slice(half * HALF, (half + 1) * HALF)
-            picked = window.indirect(lst[:, half * HALF_COLS : (half + 1) * HALF_COLS])
+        def gather(engine, dst, window, lst, cols):
+            picked = window.indirect(lst[:, cols.start // 16 : cols.stop // 16])
             if engine is nc.scalar:
                 nc.scalar.activation(dst[:, cols], picked, COPY)
             else:
                 nc.vector.tensor_copy(dst[:, cols], picked)
 
+        b_sb = sb("b_sb", [P, (PACK + 1) * H], F32)
+        nc.vector.memset(b_sb[:, PACK * H :], 0.0)
+        a_sb = [sb("a_sb%d" % j, [P, H + 16], F32) for j in range(PACK)]
+        cv = [sb("cv%d" % t, [P, 2 * H], F32) for t in range(4)]
+        for window in a_sb + cv:
+            nc.vector.memset(window[:, H:], 0.0)
+
         xs = sb("xs", [P, T], U8)
-        nc.vector.memset(xs[:].bitcast(I32), 0)
         two_t = load_list("two_t", two)
-        offs_t = load_list("offs_t", offs)
         for q in range(4):
-            nc.scalar.dma_start(xs[32 * q : 32 * q + 4, :].bitcast(I32), x_scales[0, 4 * q : 4 * q + 4, :].bitcast(I32))
+            rows = x_scales[0, 4 * q : 4 * q + 4, :].bitcast(I32)
+            nc.sync.dma_start(xs[32 * q : 32 * q + 32, :].bitcast(I32), rows.unsqueeze(0).to_broadcast([8, 4, T // 4]))
+        offs_t = load_list("offs_t", offs)
 
         def load_weight(name, w):
             halves = []
@@ -58,9 +64,9 @@ def tile_picked_momtmaxbover_none_p_kernel(tc, x_words, x_scales, wa, wb, gt, gi
                 halves.append(raw)
             return halves
 
-        wb_raw = load_weight("wb", wb)
         xw = sb("xw", [P, T], U32)
         nc.sync.dma_start(xw[:].bitcast(I32), x_words[0].rearrange("p n t -> p (n t)").bitcast(I32))
+        wb_raw = load_weight("wb", wb)
         n2_t = load_list("n2_t", n2)
         n1_t = load_list("n1_t", n1)
         wa_raw = load_weight("wa", wa)
@@ -117,29 +123,29 @@ def tile_picked_momtmaxbover_none_p_kernel(tc, x_words, x_scales, wa, wb, gt, gi
 
         two_listed = pick_scales("two_sc", two_t)
         offs_listed = pick_scales("offs_sc", offs_t)
+        two_w = pick_words("two_w", two_t)
         two_sc = deal_scales("two_sc", two_listed)
         offs_sc = deal_scales("offs_sc", offs_listed)
         wb_woven = sb("wb_woven", [P, H * PACK], BF16)
-        for h in range(2):
-            weave_weight(nc.scalar, wb_woven, wb_raw[h], h)
         wb_codes = sb("wb_codes", [P, H], U32)
         wb_scales = sb("wb_scales", [P, H], U8)
-        quantize(wb_codes[:], wb_scales[:], wb_woven[:])
-        two_w = pick_words("two_w", two_t)
-        b_ps = []
-        for j in range(PACK):
-            acc = psum.tile([P, H], F32, name="b_ps%d" % j)
-            cols = slice(j * P, (j + 1) * P)
-            product(acc[:], two_w[:, cols], two_sc[:, cols], wb_codes[:], wb_scales[:])
-            b_ps.append(acc)
-        offs_w = pick_words("offs_w", offs_t)
-        b_sb = sb("b_sb", [P, PACK, H], F32)
-        for j in range(PACK):
-            nc.scalar.copy(b_sb[:, j, :], b_ps[j][:])
+        b_ps = [psum.tile([P, H], F32, name="b_ps%d" % j) for j in range(PACK)]
+        for h in range(2):
+            weave_weight(nc.scalar, wb_woven, wb_raw[h], h)
+        for h in range(2):
+            half = slice(h * HALF, (h + 1) * HALF)
+            quantize(wb_codes[:, half], wb_scales[:, half], wb_woven[:, h * HALF * PACK : (h + 1) * HALF * PACK])
+            if h == 0:
+                offs_w = pick_words("offs_w", offs_t)
+            for j in range(PACK):
+                cols = slice(j * P, (j + 1) * P)
+                product(b_ps[j][:, half], two_w[:, cols], two_sc[:, cols], wb_codes[:, half], wb_scales[:, half])
+            for j in range(PACK):
+                nc.scalar.copy(b_sb[:, j * H + h * HALF : j * H + (h + 1) * HALF], b_ps[j][:, half])
 
         wa_woven = sb("wa_woven", [P, H * PACK], BF16)
-        for h in range(2):
-            weave_weight(nc.vector, wa_woven, wa_raw[h], h)
+        weave_weight(nc.vector, wa_woven, wa_raw[0], 0)
+        weave_weight(nc.vector, wa_woven, wa_raw[1], 1)
         wa_codes = sb("wa_codes", [P, H], U32)
         wa_scales = sb("wa_scales", [P, H], U8)
         quantize(wa_codes[:], wa_scales[:], wa_woven[:])
@@ -152,32 +158,40 @@ def tile_picked_momtmaxbover_none_p_kernel(tc, x_words, x_scales, wa, wb, gt, gi
 
         b_at = [sb("b_at%d" % j, [P, H], F32) for j in range(PACK)]
         for j in range(PACK):
-            for h in range(2):
-                gather(nc.scalar, b_at[j], b_sb[:, j, :], n2_t, h)
+            gather(nc.scalar, b_at[j], b_sb[:, j * H : (j + 2) * H], n2_t, WHOLE)
 
+        for j in range(PACK):
+            nc.vector.tensor_scalar(a_sb[j][:, :H], a_ps[j][:], gt_abs[:, j : j + 1], None, ALU.mult)
         z2_woven = sb("z2_woven", [P, H * PACK], BF16)
         nc.vector.tensor_tensor(
             z2_woven[:].rearrange("p (c e j) -> p c j e", e=4, j=PACK),
-            b_sb[:].rearrange("p j (c e) -> p c j e", e=4),
+            b_sb[:, : PACK * H].rearrange("p (j c e) -> p c j e", j=PACK, e=4),
             gi_signed[:].unsqueeze(1).unsqueeze(3).to_broadcast([P, H // 4, PACK, 4]),
             ALU.mult,
         )
-        a_sb = [sb("a_sb%d" % j, [P, H], F32) for j in range(PACK)]
-        for j in range(PACK):
-            nc.vector.tensor_scalar(a_sb[j][:], a_ps[j][:], gt_abs[:, j : j + 1], None, ALU.mult)
-        z2_codes = sb("z2_codes", [P, H], U32)
-        z2_scales = sb("z2_scales", [P, H], U8)
-        quantize(z2_codes[:], z2_scales[:], z2_woven[:])
 
         a_at = [sb("a_at%d" % j, [P, H], F32) for j in range(PACK)]
         upper = sb("upper", [P, PACK, H], F32)
         lower = sb("lower", [P, PACK, H], F32)
+        z2_codes = sb("z2_codes", [P, H], U32)
+        z2_scales = sb("z2_scales", [P, H], U8)
         for j in range(PACK):
-            nc.vector.scalar_tensor_tensor(upper[:, j, :], b_at[j][:], gt_abs[:, j : j + 1], a_sb[j][:], ALU.mult, ALU.max)
+            nc.vector.scalar_tensor_tensor(upper[:, j, :], b_at[j][:], gt_abs[:, j : j + 1], a_sb[j][:, :H], ALU.mult, ALU.max)
+            if j == 0:
+                quantize(z2_codes[:], z2_scales[:], z2_woven[:])
         for j in range(PACK):
-            for h in range(2):
-                gather(nc.scalar, a_at[j], a_sb[j][:], n1_t, h)
+            gather(nc.scalar, a_at[j], a_sb[j][:], n1_t, WHOLE)
+        for j in range(PACK - 1):
             nc.vector.scalar_tensor_tensor(lower[:, j, :], b_ps[j][:], gt_abs[:, j : j + 1], a_at[j][:], ALU.mult, ALU.min)
+
+        def of_tile(ap, t):
+            return ap.rearrange("p (c t e) -> p t c e", t=4, e=4)[:, t]
+
+        def last_lower(t):
+            j = PACK - 1
+            nc.vector.scalar_tensor_tensor(
+                of_tile(lower[:, j, :], t), of_tile(b_ps[j][:], t), gt_abs[:, j : j + 1], of_tile(a_at[j][:], t), ALU.mult, ALU.min
+            )
 
         z_woven = [sb("z_woven%d" % t, [P, P * PACK], BF16) for t in range(4)]
         z_codes = [sb("z_codes%d" % t, [P, P], U32) for t in range(4)]
@@ -198,25 +212,61 @@ def tile_picked_momtmaxbover_none_p_kernel(tc, x_words, x_scales, wa, wb, gt, gi
             product(acc[:], z_codes[t][:], z_scales[t][:], z2_codes[:], z2_scales[:])
             cv_ps.append(acc)
 
+        last_lower(0)
+        last_lower(1)
         weave_z(0)
-        for t in range(1, 4):
-            weave_z(t)
-            moments(t - 1)
+        last_lower(2)
+        moments(0)
+        last_lower(3)
+        weave_z(1)
+        weave_z(2)
+        moments(1)
+        weave_z(3)
+        moments(2)
         moments(3)
 
         out_rows = out.rearrange("(c t e) n -> t c e n", t=4, e=4)
-        on_vector = [0, 1, 2, 2]
-        for t in range(4):
-            cv = sb("cv%d" % t, [P, H], F32)
-            nc.scalar.activation(cv[:], cv_ps[t][:], COPY, scale=0.0625)
-            at3 = sb("at3_%d" % t, [P, H], F32)
-            at4 = sb("at4_%d" % t, [P, H], F32)
-            for h in range(2):
-                gather(nc.scalar, at3, cv[:], n3_t, h)
-            for h in range(2):
-                gather(nc.vector if h < on_vector[t] else nc.scalar, at4, cv[:], n4_t, h)
-            top = sb("top%d" % t, [P, H], F32)
-            nc.vector.tensor_tensor(top[:], at3[:], at4[:], ALU.max)
-            res = sb("res%d" % t, [P, H], F32)
-            nc.vector.scalar_tensor_tensor(res[:], cv_ps[t][:], -0.75 * 0.0625, top[:], ALU.mult, ALU.add)
-            nc.sync.dma_start(out_rows[t], res[:])
+        at3 = [sb("at3_%d" % t, [P, H], F32) for t in range(4)]
+        at4 = [sb("at4_%d" % t, [P, H], F32) for t in range(4)]
+        top = [sb("top%d" % t, [P, H], F32) for t in range(4)]
+        res = [sb("res%d" % t, [P, H], F32) for t in range(4)]
+
+        def leave_bank(engine, t):
+            if engine is nc.scalar:
+                nc.scalar.activation(cv[t][:, :H], cv_ps[t][:], COPY, scale=0.0625)
+            else:
+                nc.vector.tensor_scalar(cv[t][:, :H], cv_ps[t][:], 0.0625, None, ALU.mult)
+
+        def fetch(engine, t, h):
+            gather(engine, at3[t], cv[t][:], n3_t, h)
+            gather(engine, at4[t], cv[t][:], n4_t, h)
+
+        def larger(t, cols):
+            nc.vector.tensor_tensor(top[t][:, cols], at3[t][:, cols], at4[t][:, cols], ALU.max)
+
+        def finish(t, cols):
+            nc.vector.scalar_tensor_tensor(res[t][:, cols], cv_ps[t][:, cols], -0.75 * 0.0625, top[t][:, cols], ALU.mult, ALU.add)
+            nc.sync.dma_start(out_rows[t][:, :, cols], res[t][:, cols])
+
+        leave_bank(nc.scalar, 0)
+        gather(nc.scalar, at3[0], cv[0][:], n3_t, WHOLE)
+        leave_bank(nc.scalar, 1)
+        gather(nc.scalar, at4[0], cv[0][:], n4_t, WHOLE)
+        leave_bank(nc.scalar, 3)
+        fetch(nc.scalar, 1, WHOLE)
+        gather(nc.scalar, at3[3], cv[3][:], n3_t, WHOLE)
+        gather(nc.scalar, at4[3], cv[3][:], n4_t, RIGHT)
+
+        leave_bank(nc.vector, 2)
+        fetch(nc.vector, 2, WHOLE)
+        larger(0, WHOLE)
+        larger(2, WHOLE)
+        finish(0, WHOLE)
+        finish(2, WHOLE)
+        gather(nc.vector, at4[3], cv[3][:], n4_t, LEFT)
+        larger(1, WHOLE)
+        finish(1, WHOLE)
+        larger(3, LEFT)
+        larger(3, RIGHT)
+        finish(3, LEFT)
+        finish(3, RIGHT)

@@ -86,27 +86,24 @@ def tile_picked_momtmaxbover_none_p_kernel(tc, x_words, x_scales, wa, wb, gt, gi
         nc.gpsimd.tensor_tensor(gt_abs[:], gt_t[:], sign[:], ALU.mult)
         nc.gpsimd.tensor_tensor(gi_signed[:], gi_t[:], sign[:], ALU.mult)
 
-        def pick_scales(name, lst):
-            listed = sb(name + "_listed", [P, S], U8)
-            nc.vector.tensor_copy(listed[:], xs[:].indirect(lst[:]))
-            return listed
-
-        def deal_scales(name, listed):
-            dealt = sb(name + "_dealt", [P, S], U8)
-            nc.vector.tensor_copy(
-                dealt[:].rearrange("p (j m) -> p j m", j=PACK),
-                listed[:].rearrange("p (m j) -> p j m", j=PACK),
-            )
-            return dealt
+        listed = sb("listed", [P, 2 * S], U8)
+        dealt = sb("dealt", [P, 2 * S], U8)
+        nc.vector.tensor_copy(listed[:, :S], xs[:].indirect(two_t[:]))
+        nc.vector.tensor_copy(listed[:, S:], xs[:].indirect(offs_t[:]))
+        nc.vector.tensor_copy(
+            dealt[:].rearrange("p (l j m) -> p l j m", l=2, j=PACK),
+            listed[:].rearrange("p (l m j) -> p l j m", l=2, j=PACK),
+        )
+        two_sc, offs_sc = dealt[:, :S], dealt[:, S:]
 
         def pick_words(name, lst):
             dealt = sb(name, [P, S], U32)
             nc.vector.tensor_copy(dealt[:].rearrange("p (j m) -> p m j", j=PACK), xw[:].indirect(lst[:]))
             return dealt
 
-        def weave_weight(engine, woven, raw, h):
-            dst = woven[:, h * HALF * PACK : (h + 1) * HALF * PACK].rearrange("p (c e j) -> p c j e", e=4, j=PACK)
-            src = raw[:].rearrange("p j (c e) -> p c j e", e=4)
+        def weave_weight(engine, woven, raw, h, first=0, last=HALF):
+            dst = woven[:, (h * HALF + first) * PACK : (h * HALF + last) * PACK].rearrange("p (c e j) -> p c j e", e=4, j=PACK)
+            src = raw[:, :, first:last].rearrange("p j (c e) -> p c j e", e=4)
             if engine is nc.scalar:
                 nc.scalar.copy(dst, src)
             else:
@@ -121,34 +118,41 @@ def tile_picked_momtmaxbover_none_p_kernel(tc, x_words, x_scales, wa, wb, gt, gi
                 rhs=rhs_codes.bitcast(FP8X4), rhs_scale=rhs_scales, start=True, stop=True,
             )
 
-        two_listed = pick_scales("two_sc", two_t)
-        offs_listed = pick_scales("offs_sc", offs_t)
-        two_w = pick_words("two_w", two_t)
-        two_sc = deal_scales("two_sc", two_listed)
-        offs_sc = deal_scales("offs_sc", offs_listed)
-        wb_woven = sb("wb_woven", [P, H * PACK], BF16)
         wb_codes = sb("wb_codes", [P, H], U32)
         wb_scales = sb("wb_scales", [P, H], U8)
-        b_ps = [psum.tile([P, H], F32, name="b_ps%d" % j) for j in range(PACK)]
-        for h in range(2):
-            weave_weight(nc.scalar, wb_woven, wb_raw[h], h)
-        for h in range(2):
+        b_rows = b_sb[:, : PACK * H].rearrange("p (j n) -> p j n", j=PACK)
+
+        def quantize_half(codes, scales, woven, h):
             half = slice(h * HALF, (h + 1) * HALF)
-            quantize(wb_codes[:, half], wb_scales[:, half], wb_woven[:, h * HALF * PACK : (h + 1) * HALF * PACK])
-            if h == 0:
-                offs_w = pick_words("offs_w", offs_t)
-            for j in range(PACK):
-                cols = slice(j * P, (j + 1) * P)
-                product(b_ps[j][:, half], two_w[:, cols], two_sc[:, cols], wb_codes[:, half], wb_scales[:, half])
-            for j in range(PACK):
-                nc.scalar.copy(b_sb[:, j * H + h * HALF : j * H + (h + 1) * HALF], b_ps[j][:, half])
+            quantize(codes[:, half], scales[:, half], woven[:, h * HALF * PACK : (h + 1) * HALF * PACK])
+
+        def b_half(h):
+            half = slice(h * HALF, (h + 1) * HALF)
+            for pair in range(2):
+                acc = psum.tile([P, 2, HALF], F32, name="b_ps%d%d" % (h, pair))
+                for i in range(2):
+                    cols = slice((2 * pair + i) * P, (2 * pair + i + 1) * P)
+                    product(acc[:, i, :], two_w[:, cols], two_sc[:, cols], wb_codes[:, half], wb_scales[:, half])
+                nc.scalar.copy(b_rows[:, 2 * pair : 2 * pair + 2, half], acc[:])
+
+        two_w = pick_words("two_w", two_t)
+        offs_w = pick_words("offs_w", offs_t)
+        wb_woven = sb("wb_woven", [P, H * PACK], BF16)
+        weave_weight(nc.scalar, wb_woven, wb_raw[0], 0)
+        weave_weight(nc.scalar, wb_woven, wb_raw[1], 1, 0, HALF // 2)
+        quantize_half(wb_codes, wb_scales, wb_woven, 0)
+        weave_weight(nc.vector, wb_woven, wb_raw[1], 1, HALF // 2, HALF)
+        b_half(0)
+        quantize_half(wb_codes, wb_scales, wb_woven, 1)
+        b_half(1)
 
         wa_woven = sb("wa_woven", [P, H * PACK], BF16)
-        weave_weight(nc.vector, wa_woven, wa_raw[0], 0)
-        weave_weight(nc.vector, wa_woven, wa_raw[1], 1)
         wa_codes = sb("wa_codes", [P, H], U32)
         wa_scales = sb("wa_scales", [P, H], U8)
-        quantize(wa_codes[:], wa_scales[:], wa_woven[:])
+        for h in range(2):
+            weave_weight(nc.vector, wa_woven, wa_raw[h], h)
+        for h in range(2):
+            quantize_half(wa_codes, wa_scales, wa_woven, h)
         a_ps = []
         for j in range(PACK):
             acc = psum.tile([P, H], F32, name="a_ps%d" % j, tag="bank%d" % j)
@@ -160,15 +164,20 @@ def tile_picked_momtmaxbover_none_p_kernel(tc, x_words, x_scales, wa, wb, gt, gi
         for j in range(PACK):
             gather(nc.scalar, b_at[j], b_sb[:, j * H : (j + 2) * H], n2_t, WHOLE)
 
+        z2_woven = sb("z2_woven", [P, H * PACK], BF16)
+
+        def weave_z2(h):
+            nc.vector.tensor_tensor(
+                z2_woven[:, h * HALF * PACK : (h + 1) * HALF * PACK].rearrange("p (c e j) -> p c j e", e=4, j=PACK),
+                b_rows[:, :, h * HALF : (h + 1) * HALF].rearrange("p j (c e) -> p c j e", e=4),
+                gi_signed[:].unsqueeze(1).unsqueeze(3).to_broadcast([P, HALF // 4, PACK, 4]),
+                ALU.mult,
+            )
+
+        weave_z2(0)
         for j in range(PACK):
             nc.vector.tensor_scalar(a_sb[j][:, :H], a_ps[j][:], gt_abs[:, j : j + 1], None, ALU.mult)
-        z2_woven = sb("z2_woven", [P, H * PACK], BF16)
-        nc.vector.tensor_tensor(
-            z2_woven[:].rearrange("p (c e j) -> p c j e", e=4, j=PACK),
-            b_sb[:, : PACK * H].rearrange("p (j c e) -> p c j e", j=PACK, e=4),
-            gi_signed[:].unsqueeze(1).unsqueeze(3).to_broadcast([P, H // 4, PACK, 4]),
-            ALU.mult,
-        )
+        weave_z2(1)
 
         a_at = [sb("a_at%d" % j, [P, H], F32) for j in range(PACK)]
         upper = sb("upper", [P, PACK, H], F32)
@@ -182,7 +191,7 @@ def tile_picked_momtmaxbover_none_p_kernel(tc, x_words, x_scales, wa, wb, gt, gi
         for j in range(PACK):
             gather(nc.scalar, a_at[j], a_sb[j][:], n1_t, WHOLE)
         for j in range(PACK - 1):
-            nc.vector.scalar_tensor_tensor(lower[:, j, :], b_ps[j][:], gt_abs[:, j : j + 1], a_at[j][:], ALU.mult, ALU.min)
+            nc.vector.scalar_tensor_tensor(lower[:, j, :], b_rows[:, j, :], gt_abs[:, j : j + 1], a_at[j][:], ALU.mult, ALU.min)
 
         def of_tile(ap, t):
             return ap.rearrange("p (c t e) -> p t c e", t=4, e=4)[:, t]
@@ -190,7 +199,7 @@ def tile_picked_momtmaxbover_none_p_kernel(tc, x_words, x_scales, wa, wb, gt, gi
         def last_lower(t):
             j = PACK - 1
             nc.vector.scalar_tensor_tensor(
-                of_tile(lower[:, j, :], t), of_tile(b_ps[j][:], t), gt_abs[:, j : j + 1], of_tile(a_at[j][:], t), ALU.mult, ALU.min
+                of_tile(lower[:, j, :], t), of_tile(b_rows[:, j, :], t), gt_abs[:, j : j + 1], of_tile(a_at[j][:], t), ALU.mult, ALU.min
             )
 
         z_woven = [sb("z_woven%d" % t, [P, P * PACK], BF16) for t in range(4)]

from contextlib import ExitStack

import concourse.mybir as mybir

K, T, S, H = 512, 2048, 512, 512
FLOPS = 3 * 2 * 512 * 512 * 512

F32 = mybir.dt.float32
BF16 = mybir.dt.bfloat16
I32 = mybir.dt.int32
U32 = mybir.dt.uint32
U16 = mybir.dt.uint16
U8 = mybir.dt.uint8
FP8X4 = mybir.dt.float8_e4m3fn_x4
ALU = mybir.AluOpType
COPY = mybir.ActivationFunctionType.Copy

P = 128
PACK = 4
HALF = 256
WHOLE, LEFT, RIGHT = slice(0, H), slice(0, HALF), slice(HALF, H)


def tile_picked_momtmaxbover_none_p_kernel(tc, x_words, x_scales, wa, wb, gt, gi, offs, two, n1, n2, n3, n4, out):
    nc = tc.nc
    with ExitStack() as ctx:
        keep = ctx.enter_context(tc.tile_pool(name="keep", bufs=1))
        psum = ctx.enter_context(tc.psum_pool(name="psum", bufs=1))

        def sb(name, shape, dtype):
            return keep.tile(shape, dtype, name=name, align_bytes=64)

        def load_list(name, src):
            t = keep.tile([P, S // 16], U16, name=name)
            nc.sync.dma_start(t[:], src)
            return t

        def gather(engine, dst, window, lst, cols):
            picked = window.indirect(lst[:, cols.start // 16 : cols.stop // 16])
            if engine is nc.scalar:
                nc.scalar.activation(dst[:, cols], picked, COPY)
            else:
                nc.vector.tensor_copy(dst[:, cols], picked)

        b_sb = sb("b_sb", [P, (PACK + 1) * H], F32)
        nc.vector.memset(b_sb[:, PACK * H :], 0.0)
        a_sb = [sb("a_sb%d" % j, [P, H + 16], F32) for j in range(PACK)]
        cv = [sb("cv%d" % t, [P, 2 * H], F32) for t in range(4)]
        for window in a_sb + cv:
            nc.vector.memset(window[:, H:], 0.0)

        xs = sb("xs", [P, T], U8)
        two_t = load_list("two_t", two)
        for q in range(4):
            rows = x_scales[0, 4 * q : 4 * q + 4, :].bitcast(I32)
            nc.sync.dma_start(xs[32 * q : 32 * q + 32, :].bitcast(I32), rows.unsqueeze(0).to_broadcast([8, 4, T // 4]))
        offs_t = load_list("offs_t", offs)

        def load_weight(name, w):
            halves = []
            for h in range(2):
                raw = sb(name + "_raw%d" % h, [P, PACK, HALF], F32)
                nc.sync.dma_start(raw[:], w.rearrange("(p j) n -> p j n", j=PACK)[:, :, h * HALF : (h + 1) * HALF])
                halves.append(raw)
            return halves

        xw = sb("xw", [P, T], U32)
        nc.sync.dma_start(xw[:].bitcast(I32), x_words[0].rearrange("p n t -> p (n t)").bitcast(I32))
        wb_raw = load_weight("wb", wb)
        n2_t = load_list("n2_t", n2)
        n1_t = load_list("n1_t", n1)
        wa_raw = load_weight("wa", wa)
        gt_t = sb("gt_t", [P, PACK], F32)
        gi_t = sb("gi_t", [P, PACK], F32)
        nc.scalar.dma_start(gt_t[:], gt.rearrange("(p j) o -> p (j o)", j=PACK))
        nc.scalar.dma_start(gi_t[:], gi.rearrange("(p j) o -> p (j o)", j=PACK))
        n3_t = load_list("n3_t", n3)
        n4_t = load_list("n4_t", n4)

        twice = sb("twice", [P, PACK], F32)
        sign = sb("sign", [P, PACK], F32)
        gt_abs = sb("gt_abs", [P, PACK], F32)
        gi_signed = sb("gi_signed", [P, PACK], F32)
        nc.gpsimd.tensor_scalar(twice[:], gt_t[:], 0.0, 2.0, ALU.is_ge, ALU.mult)
        nc.gpsimd.tensor_scalar(sign[:], twice[:], 1.0, -1.0, ALU.mult, ALU.add)
        nc.gpsimd.tensor_tensor(gt_abs[:], gt_t[:], sign[:], ALU.mult)
        nc.gpsimd.tensor_tensor(gi_signed[:], gi_t[:], sign[:], ALU.mult)

        listed = sb("listed", [P, 2 * S], U8)
        dealt = sb("dealt", [P, 2 * S], U8)
        nc.vector.tensor_copy(listed[:, :S], xs[:].indirect(two_t[:]))
        nc.vector.tensor_copy(listed[:, S:], xs[:].indirect(offs_t[:]))
        nc.vector.tensor_copy(
            dealt[:].rearrange("p (l j m) -> p l j m", l=2, j=PACK),
            listed[:].rearrange("p (l m j) -> p l j m", l=2, j=PACK),
        )
        two_sc, offs_sc = dealt[:, :S], dealt[:, S:]

        def pick_words(name, lst):
            dealt = sb(name, [P, S], U32)
            nc.vector.tensor_copy(dealt[:].rearrange("p (j m) -> p m j", j=PACK), xw[:].indirect(lst[:]))
            return dealt

        def weave_weight(engine, woven, raw, h, first=0, last=HALF):
            dst = woven[:, (h * HALF + first) * PACK : (h * HALF + last) * PACK].rearrange("p (c e j) -> p c j e", e=4, j=PACK)
            src = raw[:, :, first:last].rearrange("p j (c e) -> p c j e", e=4)
            if engine is nc.scalar:
                nc.scalar.copy(dst, src)
            else:
                nc.vector.tensor_copy(dst, src)

        def quantize(codes, scales, woven):
            nc.vector.quantize_mx(out=codes.bitcast(FP8X4), scales=scales, in_=woven)

        def product(acc, lhs_codes, lhs_scales, rhs_codes, rhs_scales):
            nc.tensor.matmul_mx(
                out=acc, lhsT=lhs_codes.bitcast(FP8X4), lhsT_scale=lhs_scales,
                rhs=rhs_codes.bitcast(FP8X4), rhs_scale=rhs_scales, start=True, stop=True,
            )

        wb_codes = sb("wb_codes", [P, H], U32)
        wb_scales = sb("wb_scales", [P, H], U8)
        b_rows = b_sb[:, : PACK * H].rearrange("p (j n) -> p j n", j=PACK)

        def quantize_half(codes, scales, woven, h):
            half = slice(h * HALF, (h + 1) * HALF)
            quantize(codes[:, half], scales[:, half], woven[:, h * HALF * PACK : (h + 1) * HALF * PACK])

        def b_half(h):
            half = slice(h * HALF, (h + 1) * HALF)
            for pair in range(2):
                acc = psum.tile([P, 2, HALF], F32, name="b_ps%d%d" % (h, pair))
                for i in range(2):
                    cols = slice((2 * pair + i) * P, (2 * pair + i + 1) * P)
                    product(acc[:, i, :], two_w[:, cols], two_sc[:, cols], wb_codes[:, half], wb_scales[:, half])
                nc.scalar.copy(b_rows[:, 2 * pair : 2 * pair + 2, half], acc[:])

        two_w = pick_words("two_w", two_t)
        offs_w = pick_words("offs_w", offs_t)
        wb_woven = sb("wb_woven", [P, H * PACK], BF16)
        weave_weight(nc.scalar, wb_woven, wb_raw[0], 0)
        weave_weight(nc.scalar, wb_woven, wb_raw[1], 1, 0, HALF // 2)
        quantize_half(wb_codes, wb_scales, wb_woven, 0)
        weave_weight(nc.vector, wb_woven, wb_raw[1], 1, HALF // 2, HALF)
        b_half(0)
        quantize_half(wb_codes, wb_scales, wb_woven, 1)
        b_half(1)

        wa_woven = sb("wa_woven", [P, H * PACK], BF16)
        wa_codes = sb("wa_codes", [P, H], U32)
        wa_scales = sb("wa_scales", [P, H], U8)
        for h in range(2):
            weave_weight(nc.vector, wa_woven, wa_raw[h], h)
        for h in range(2):
            quantize_half(wa_codes, wa_scales, wa_woven, h)
        a_ps = []
        for j in range(PACK):
            acc = psum.tile([P, H], F32, name="a_ps%d" % j, tag="bank%d" % j)
            cols = slice(j * P, (j + 1) * P)
            product(acc[:], offs_w[:, cols], offs_sc[:, cols], wa_codes[:], wa_scales[:])
            a_ps.append(acc)

        b_at = [sb("b_at%d" % j, [P, H], F32) for j in range(PACK)]
        for j in range(PACK):
            gather(nc.scalar, b_at[j], b_sb[:, j * H : (j + 2) * H], n2_t, WHOLE)

        z2_woven = sb("z2_woven", [P, H * PACK], BF16)

        def weave_z2(h):
            nc.vector.tensor_tensor(
                z2_woven[:, h * HALF * PACK : (h + 1) * HALF * PACK].rearrange("p (c e j) -> p c j e", e=4, j=PACK),
                b_rows[:, :, h * HALF : (h + 1) * HALF].rearrange("p j (c e) -> p c j e", e=4),
                gi_signed[:].unsqueeze(1).unsqueeze(3).to_broadcast([P, HALF // 4, PACK, 4]),
                ALU.mult,
            )

        weave_z2(0)
        for j in range(PACK):
            nc.vector.tensor_scalar(a_sb[j][:, :H], a_ps[j][:], gt_abs[:, j : j + 1], None, ALU.mult)
        weave_z2(1)

        a_at = [sb("a_at%d" % j, [P, H], F32) for j in range(PACK)]
        upper = sb("upper", [P, PACK, H], F32)
        lower = sb("lower", [P, PACK, H], F32)
        z2_codes = sb("z2_codes", [P, H], U32)
        z2_scales = sb("z2_scales", [P, H], U8)
        for j in range(PACK):
            nc.vector.scalar_tensor_tensor(upper[:, j, :], b_at[j][:], gt_abs[:, j : j + 1], a_sb[j][:, :H], ALU.mult, ALU.max)
            if j == 0:
                quantize(z2_codes[:], z2_scales[:], z2_woven[:])
        for j in range(PACK):
            gather(nc.scalar, a_at[j], a_sb[j][:], n1_t, WHOLE)
        for j in range(PACK - 1):
            nc.vector.scalar_tensor_tensor(lower[:, j, :], b_rows[:, j, :], gt_abs[:, j : j + 1], a_at[j][:], ALU.mult, ALU.min)

        def of_tile(ap, t):
            return ap.rearrange("p (c t e) -> p t c e", t=4, e=4)[:, t]

        def last_lower(t):
            j = PACK - 1
            nc.vector.scalar_tensor_tensor(
                of_tile(lower[:, j, :], t), of_tile(b_rows[:, j, :], t), gt_abs[:, j : j + 1], of_tile(a_at[j][:], t), ALU.mult, ALU.min
            )

        z_woven = [sb("z_woven%d" % t, [P, P * PACK], BF16) for t in range(4)]
        z_codes = [sb("z_codes%d" % t, [P, P], U32) for t in range(4)]
        z_scales = [sb("z_scales%d" % t, [P, P], U8) for t in range(4)]
        cv_ps = []

        def weave_z(t):
            nc.vector.tensor_tensor(
                z_woven[t][:].rearrange("p (c e j) -> p c j e", e=4, j=PACK),
                upper[:].rearrange("p j (c t e) -> p t c j e", t=4, e=4)[:, t],
                lower[:].rearrange("p j (c t e) -> p t c j e", t=4, e=4)[:, t],
                ALU.subtract,
            )

        def moments(t):
            quantize(z_codes[t][:], z_scales[t][:], z_woven[t][:])
            acc = psum.tile([P, H], F32, name="cv_ps%d" % t, tag="bank%d" % t)
            product(acc[:], z_codes[t][:], z_scales[t][:], z2_codes[:], z2_scales[:])
            cv_ps.append(acc)

        last_lower(0)
        last_lower(1)
        weave_z(0)
        last_lower(2)
        moments(0)
        last_lower(3)
        weave_z(1)
        weave_z(2)
        moments(1)
        weave_z(3)
        moments(2)
        moments(3)

        out_rows = out.rearrange("(c t e) n -> t c e n", t=4, e=4)
        at3 = [sb("at3_%d" % t, [P, H], F32) for t in range(4)]
        at4 = [sb("at4_%d" % t, [P, H], F32) for t in range(4)]
        top = [sb("top%d" % t, [P, H], F32) for t in range(4)]
        res = [sb("res%d" % t, [P, H], F32) for t in range(4)]

        def leave_bank(engine, t):
            if engine is nc.scalar:
                nc.scalar.activation(cv[t][:, :H], cv_ps[t][:], COPY, scale=0.0625)
            else:
                nc.vector.tensor_scalar(cv[t][:, :H], cv_ps[t][:], 0.0625, None, ALU.mult)

        def fetch(engine, t, h):
            gather(engine, at3[t], cv[t][:], n3_t, h)
            gather(engine, at4[t], cv[t][:], n4_t, h)

        def larger(t, cols):
            nc.vector.tensor_tensor(top[t][:, cols], at3[t][:, cols], at4[t][:, cols], ALU.max)

        def finish(t, cols):
            nc.vector.scalar_tensor_tensor(res[t][:, cols], cv_ps[t][:, cols], -0.75 * 0.0625, top[t][:, cols], ALU.mult, ALU.add)
            nc.sync.dma_start(out_rows[t][:, :, cols], res[t][:, cols])

        leave_bank(nc.scalar, 0)
        gather(nc.scalar, at3[0], cv[0][:], n3_t, WHOLE)
        leave_bank(nc.scalar, 1)
        gather(nc.scalar, at4[0], cv[0][:], n4_t, WHOLE)
        leave_bank(nc.scalar, 3)
        fetch(nc.scalar, 1, WHOLE)
        gather(nc.scalar, at3[3], cv[3][:], n3_t, WHOLE)
        gather(nc.scalar, at4[3], cv[3][:], n4_t, RIGHT)

        leave_bank(nc.vector, 2)
        fetch(nc.vector, 2, WHOLE)
        larger(0, WHOLE)
        larger(2, WHOLE)
        finish(0, WHOLE)
        finish(2, WHOLE)
        gather(nc.vector, at4[3], cv[3][:], n4_t, LEFT)
        larger(1, WHOLE)
        finish(1, WHOLE)
        larger(3, LEFT)
        larger(3, RIGHT)
        finish(3, LEFT)
        finish(3, RIGHT)
